import numpy as np
import ml_dtypes


def mxq(x, axis, fmt="e4m3"):
    dtype, down = {"e4m3": (ml_dtypes.float8_e4m3fn, 7), "e5m2": (ml_dtypes.float8_e5m2, 14)}[fmt]
    v = np.moveaxis(np.asarray(x, np.float32).astype(ml_dtypes.bfloat16).astype(np.float64), axis, -1)
    blocks = v.reshape(v.shape[:-1] + (-1, 32))
    amax = np.abs(blocks).max(-1, keepdims=True)
    byte = np.maximum(np.where(amax > 0, np.frexp(amax)[1] - 1 + 127, 0) - down, 1)
    scale = np.exp2(byte - 127.0)
    codes = (blocks / scale).astype(np.float32).astype(dtype).astype(np.float64)
    return np.moveaxis((codes * scale).reshape(v.shape), -1, axis)


WIDE = False


def mx_kscale(k):
    if not WIDE:
        return np.ones(k)
    levels = np.array([10, -10, 5, -5, 0])
    if k % 512:
        return np.exp2(np.random.permutation(np.resize(levels, k // 32))).repeat(32)
    a = np.empty((k // 512, 16))
    for p in range(k // 512):
        a[p, :8] = np.random.permutation(np.resize(levels, 8))
        for g in range(8):
            far = levels[np.abs(levels - a[p, g]) >= 10]
            a[p, g + 8] = far[np.random.randint(len(far))]
    return np.exp2(a.ravel()).repeat(32)


def f64(x):
    return np.asarray(x).astype(np.float64)


def striped(idx):
    return np.tile(idx.reshape(-1, 16).T, (8, 1)).astype(np.uint16)


def unstriped(offs):
    return offs[:16].T.reshape(-1).astype(np.int64)


def pack_weight(w):
    k, n = w.shape
    w = f64(np.asarray(w, np.float32).astype(ml_dtypes.bfloat16)).reshape(k // 32, 32, n)
    amax = np.abs(w).max(1)
    byte = np.clip(np.where(amax > 0, np.frexp(amax)[1] - 1 + 127 - 7, 1), 1, 254)
    scaled = (w * np.exp2(127.0 - byte)[:, None, :]).reshape(k, n).astype(np.float32)
    words = np.ascontiguousarray(scaled.reshape(k // 512, 128, 4, n).transpose(0, 1, 3, 2)).astype(ml_dtypes.float8_e4m3fn).view(np.uint8)
    return words, np.ascontiguousarray(byte.astype(np.uint8).reshape(k // 512, 16, n))


def unpack_weight(words, scales):
    g, p, n, _ = words.shape
    vals = np.ascontiguousarray(words).view(ml_dtypes.float8_e4m3fn).astype(np.float64) * np.repeat(np.exp2(scales.astype(np.float64) - 127.0), 8, axis=1)[..., None]
    return vals.transpose(0, 1, 3, 2).reshape(g * 512, n)


K, T, S, D, H, N = 512, 2048, 1024, 4, 512, 256


def setup_inputs():
    n = np.random.standard_normal
    s = mx_kscale(K)[:, None]
    u = mx_kscale(H)
    packed_xT = pack_weight(n((K, T)) * s)
    packed_w2 = pack_weight(n((H, N)) / np.sqrt(H) / u[:, None])
    return {
        "x_words": packed_xT[0],
        "x_scales": packed_xT[1],
        "w1": (n((K, H)) / np.sqrt(K) / s * u).astype(np.float32),
        "w2_words": packed_w2[0],
        "w2_scales": packed_w2[1],
        "taps": (n((H, D)) / np.sqrt(D)).astype(np.float32),
        "offs": striped(np.random.permutation(T)[:S]),
    }


def reference(x_words, x_scales, w1, w2_words, w2_scales, taps, offs):
    xq = unpack_weight(x_words, x_scales)[:, unstriped(offs)]
    h = mxq(f64(w1), 0, "e4m3").T @ xq
    z = f64(taps)[:, 0:1] * h + f64(taps)[:, 1:2] * (np.pad(h, ((0, 0), (1, 0)))[:, :S]) + f64(taps)[:, 2:3] * (np.pad(h, ((0, 0), (2, 0)))[:, :S]) + f64(taps)[:, 3:4] * (np.pad(h, ((0, 0), (3, 0)))[:, :S])
    return unpack_weight(w2_words, w2_scales).T @ mxq(z, 0, "e4m3")

@@ -1,0 +1,158 @@
+from contextlib import ExitStack
+
+import concourse.mybir as mybir
+
+K, T, S, TAPS, H, N = 512, 2048, 1024, 4, 512, 256
+FLOPS = 2 * K * H * S + 2 * H * N * S
+
+F32 = mybir.dt.float32
+BF16 = mybir.dt.bfloat16
+I32 = mybir.dt.int32
+U32 = mybir.dt.uint32
+U16 = mybir.dt.uint16
+U8 = mybir.dt.uint8
+FP8X4 = mybir.dt.float8_e4m3fn_x4
+COPY = mybir.ActivationFunctionType.Copy
+MULT = mybir.AluOpType.mult
+ADD = mybir.AluOpType.add
+
+P = 128
+PACK = 4
+BANK = 512
+GATHER = 256
+CHUNKS = [256,256,256,128,128]
+GPSIMD_CHUNKS = 4
+W1_PIECES = [256,128,128]
+ROW = S + 8
+
+
+def load_scale_rows(nc, plane, rows):
+    for q in range(4):
+        nc.sync.dma_start(out=plane[32 * q : 32 * q + 4, :].bitcast(I32), in_=rows[4 * q : 4 * q + 4, :].bitcast(I32))
+
+
+def tile_picked_dconv_none_p_kernel(tc, x_words, x_scales, w1, w2_words, w2_scales, taps, offs, out):
+    nc = tc.nc
+    with ExitStack() as ctx:
+        keep = ctx.enter_context(tc.tile_pool(name="keep", bufs=1))
+        zpool = ctx.enter_context(tc.tile_pool(name="zpool", bufs=1))
+        ring = ctx.enter_context(tc.tile_pool(name="ring", bufs=2))
+        picks = ctx.enter_context(tc.tile_pool(name="picks", bufs=3))
+        hpsum = ctx.enter_context(tc.psum_pool(name="hpsum", bufs=6))
+        opsum = ctx.enter_context(tc.psum_pool(name="opsum", bufs=2))
+
+        offsets = keep.tile([P, S // 16], U16, name="offsets")
+        x_table = keep.tile([P, T], I32, name="x_table", align_bytes=64)
+        x_plane = keep.tile([P, T], U8, name="x_plane", align_bytes=64)
+        w2_codes = keep.tile([P, N], I32, name="w2_codes", align_bytes=64)
+        w2_plane = keep.tile([P, N], U8, name="w2_plane", align_bytes=64)
+        tap = keep.tile([P, PACK, TAPS], F32, name="tap")
+        zeros = keep.tile([P, 2, PACK, 1], F32, name="zeros")
+        odd = keep.tile([P, 2, PACK, ROW], F32, name="odd")
+        far = keep.tile([P, PACK, ROW], F32, name="far")
+
+        nc.vector.memset(x_plane[:].bitcast(I32), 0)
+        nc.vector.memset(zeros[:], 0.0)
+        nc.vector.memset(w2_plane[:].bitcast(I32), 0)
+        nc.vector.memset(far[:, :, 0:2], 0.0)
+        nc.scalar.activation(out=odd[:, :, :, 0:1], in_=zeros[:], func=COPY)
+
+        nc.sync.dma_start(offsets[:], offs)
+        nc.sync.dma_start(out=x_table[:], in_=x_words[0].rearrange("p n r -> p (n r)").bitcast(I32))
+        load_scale_rows(nc, x_plane, x_scales[0])
+
+        w1_rows = w1.rearrange("(p j) c -> p j c", j=PACK)
+        w1_grouped = keep.tile([P, PACK, P, PACK], BF16, name="w1_grouped", align_bytes=64)
+        c0 = 0
+        for i, width in enumerate(W1_PIECES):
+            raw = keep.tile([P, PACK, width], F32, name="w1_raw%d" % i)
+            nc.sync.dma_start(out=raw[:], in_=w1_rows[:, :, c0 : c0 + width])
+            nc.scalar.activation(
+                out=w1_grouped[:, :, c0 // PACK : (c0 + width) // PACK, :].rearrange("p t m j -> p m t j"),
+                in_=raw[:].rearrange("p j (m t) -> p m t j", t=PACK),
+                func=COPY,
+            )
+            c0 = c0 + width
+        nc.sync.dma_start(out=tap[:], in_=taps.rearrange("(p t) d -> p t d", t=PACK))
+        nc.sync.dma_start(out=w2_codes[:], in_=w2_words[0].rearrange("p n r -> p (n r)").bitcast(I32))
+        load_scale_rows(nc, w2_plane, w2_scales[0])
+
+        picked = []
+
+        def gather(g):
+            words = picks.tile([P, GATHER], U32, name="picked_words", align_bytes=64)
+            plane = picks.tile([P, GATHER], U8, name="picked_plane", align_bytes=64)
+            entries = offsets[:, g * GATHER // 16 : (g + 1) * GATHER // 16]
+            nc.vector.tensor_copy(out=words[:], in_=x_table[:].bitcast(U32).indirect(entries))
+            nc.vector.tensor_copy(out=plane[:], in_=x_plane[:].indirect(entries))
+            picked.append((words, plane))
+
+        gather(0)
+        w1_codes, w1_planes = [], []
+        for t in range(PACK):
+            codes = keep.tile([P, P], U32, name="w1_codes%d" % t, align_bytes=64)
+            plane = keep.tile([P, P], U8, name="w1_plane%d" % t, align_bytes=64)
+            nc.vector.quantize_mx(out=codes[:].bitcast(FP8X4), scales=plane[:], in_=w1_grouped[:, t, :, :].rearrange("p m j -> p (m j)"))
+            w1_codes.append(codes)
+            w1_planes.append(plane)
+
+        def convolve(j0, n):
+            words, plane = picked[j0 // GATHER]
+            cols = slice(j0 % GATHER, j0 % GATHER + n)
+            near = ring.tile([P, PACK, n], F32, name="near")
+            for t in range(PACK):
+                h = hpsum.tile([P, BANK], F32, name="h")
+                nc.tensor.matmul_mx(
+                    out=h[:, 0:n],
+                    lhsT=w1_codes[t][:].bitcast(FP8X4),
+                    lhsT_scale=w1_planes[t][:],
+                    rhs=words[:, cols].bitcast(FP8X4),
+                    rhs_scale=plane[:, cols],
+                    start=True,
+                    stop=True,
+                )
+                for u in range(2):
+                    nc.scalar.activation(out=odd[:, u, t, j0 + 1 : j0 + 1 + n], in_=h[:, 0:n], func=COPY, scale=tap[:, t, 2 * u + 1 : 2 * u + 2])
+                nc.vector.scalar_tensor_tensor(out=near[:, t, :], in0=h[:, 0:n], scalar=tap[:, t, 0:1], in1=odd[:, 0, t, j0 : j0 + n], op0=MULT, op1=ADD)
+                nc.vector.scalar_tensor_tensor(out=far[:, t, j0 + 2 : j0 + 2 + n], in0=h[:, 0:n], scalar=tap[:, t, 2:3], in1=odd[:, 1, t, j0 : j0 + n], op0=MULT, op1=ADD)
+            return near
+
+        def join(j0, n, near, engine):
+            z = zpool.tile([P, n, PACK], BF16, name="z", align_bytes=64)
+            engine.tensor_tensor(
+                out=z[:].rearrange("p (c i) t -> p c t i", i=4),
+                in0=near[:].rearrange("p t (c i) -> p c t i", i=4),
+                in1=far[:, :, j0 : j0 + n].rearrange("p t (c i) -> p c t i", i=4),
+                op=ADD,
+            )
+            return z
+
+        def project(j0, n, z):
+            codes = ring.tile([P, n], U32, name="z_codes", align_bytes=64)
+            plane = ring.tile([P, n], U8, name="z_plane", align_bytes=64)
+            nc.vector.quantize_mx(out=codes[:].bitcast(FP8X4), scales=plane[:], in_=z[:].rearrange("p j t -> p (j t)"))
+            acc = opsum.tile([P, N // P, BANK // 2], F32, name="acc")
+            for m in range(N // P):
+                nc.tensor.matmul_mx(
+                    out=acc[:, m, 0:n],
+                    lhsT=w2_codes[:, m * P : (m + 1) * P].bitcast(FP8X4),
+                    lhsT_scale=w2_plane[:, m * P : (m + 1) * P],
+                    rhs=codes[:].bitcast(FP8X4),
+                    rhs_scale=plane[:],
+                    start=True,
+                    stop=True,
+                )
+            result = ring.tile([P, N // P, n], F32, name="result")
+            nc.scalar.activation(out=result[:], in_=acc[:, :, 0:n], func=COPY)
+            nc.sync.dma_start(out=out.rearrange("(m p) j -> p m j", p=P)[:, :, j0 : j0 + n], in_=result[:])
+
+        starts = [sum(CHUNKS[:c]) for c in range(len(CHUNKS))]
+        waiting = None
+        for c, (j0, n) in enumerate(zip(starts, CHUNKS)):
+            if len(picked) < S // GATHER:
+                gather(len(picked))
+            near = convolve(j0, n)
+            if waiting is not None:
+                project(*waiting)
+            waiting = (j0, n, join(j0, n, near, nc.gpsimd if c < GPSIMD_CHUNKS else nc.vector))
+        project(*waiting)

@@ -19,9 +19,10 @@ ADD = mybir.AluOpType.add
 P = 128
 PACK = 4
 BANK = 512
-GATHER = 256
-CHUNKS = [256,256,256,128,128]
-GPSIMD_CHUNKS = 4
+EARLY = 640
+CHUNKS = [128,256,256,256,128]
+GPSIMD_SHARE = [128,176,176,80,0]
+OVERLAP = 4
 W1_PIECES = [256,128,128]
 ROW = S + 8
 
@@ -35,9 +36,8 @@ def tile_picked_dconv_none_p_kernel(tc, x_words, x_scales, w1, w2_words, w2_scal
     nc = tc.nc
     with ExitStack() as ctx:
         keep = ctx.enter_context(tc.tile_pool(name="keep", bufs=1))
-        zpool = ctx.enter_context(tc.tile_pool(name="zpool", bufs=1))
+        zpool = ctx.enter_context(tc.tile_pool(name="zpool", bufs=2))
         ring = ctx.enter_context(tc.tile_pool(name="ring", bufs=2))
-        picks = ctx.enter_context(tc.tile_pool(name="picks", bufs=3))
         hpsum = ctx.enter_context(tc.psum_pool(name="hpsum", bufs=6))
         opsum = ctx.enter_context(tc.psum_pool(name="opsum", bufs=2))
 
@@ -49,22 +49,17 @@ def tile_picked_dconv_none_p_kernel(tc, x_words, x_scales, w1, w2_words, w2_scal
         tap = keep.tile([P, PACK, TAPS], F32, name="tap")
         zeros = keep.tile([P, 2, PACK, 1], F32, name="zeros")
         odd = keep.tile([P, 2, PACK, ROW], F32, name="odd")
-        far = keep.tile([P, PACK, ROW], F32, name="far")
 
         nc.vector.memset(x_plane[:].bitcast(I32), 0)
         nc.vector.memset(zeros[:], 0.0)
         nc.vector.memset(w2_plane[:].bitcast(I32), 0)
-        nc.vector.memset(far[:, :, 0:2], 0.0)
         nc.scalar.activation(out=odd[:, :, :, 0:1], in_=zeros[:], func=COPY)
 
-        nc.sync.dma_start(offsets[:], offs)
-        nc.sync.dma_start(out=x_table[:], in_=x_words[0].rearrange("p n r -> p (n r)").bitcast(I32))
-        load_scale_rows(nc, x_plane, x_scales[0])
-
         w1_rows = w1.rearrange("(p j) c -> p j c", j=PACK)
-        w1_grouped = keep.tile([P, PACK, P, PACK], BF16, name="w1_grouped", align_bytes=64)
-        c0 = 0
-        for i, width in enumerate(W1_PIECES):
+        w1_grouped = keep.tile([P, PACK, P, PACK], BF16, name="w1_grouped", tag="shared", align_bytes=64)
+
+        def load_w1_piece(i):
+            c0, width = sum(W1_PIECES[:i]), W1_PIECES[i]
             raw = keep.tile([P, PACK, width], F32, name="w1_raw%d" % i)
             nc.sync.dma_start(out=raw[:], in_=w1_rows[:, :, c0 : c0 + width])
             nc.scalar.activation(
@@ -72,22 +67,25 @@ def tile_picked_dconv_none_p_kernel(tc, x_words, x_scales, w1, w2_words, w2_scal
                 in_=raw[:].rearrange("p j (m t) -> p m t j", t=PACK),
                 func=COPY,
             )
-            c0 = c0 + width
+
+        nc.sync.dma_start(offsets[:], offs)
         nc.sync.dma_start(out=tap[:], in_=taps.rearrange("(p t) d -> p t d", t=PACK))
+        load_w1_piece(0)
+        load_scale_rows(nc, x_plane, x_scales[0])
+        nc.sync.dma_start(out=x_table[:], in_=x_words[0].rearrange("p n r -> p (n r)").bitcast(I32))
+        for i in range(1, len(W1_PIECES)):
+            load_w1_piece(i)
         nc.sync.dma_start(out=w2_codes[:], in_=w2_words[0].rearrange("p n r -> p (n r)").bitcast(I32))
         load_scale_rows(nc, w2_plane, w2_scales[0])
 
-        picked = []
+        picked_plane = keep.tile([P, S], U8, name="picked_plane", align_bytes=64)
+        nc.vector.tensor_copy(out=picked_plane[:], in_=x_plane[:].indirect(offsets[:]))
 
-        def gather(g):
-            words = picks.tile([P, GATHER], U32, name="picked_words", align_bytes=64)
-            plane = picks.tile([P, GATHER], U8, name="picked_plane", align_bytes=64)
-            entries = offsets[:, g * GATHER // 16 : (g + 1) * GATHER // 16]
-            nc.vector.tensor_copy(out=words[:], in_=x_table[:].bitcast(U32).indirect(entries))
-            nc.vector.tensor_copy(out=plane[:], in_=x_plane[:].indirect(entries))
-            picked.append((words, plane))
+        def gather(words, j0, n):
+            nc.vector.tensor_copy(out=words[:], in_=x_table[:].bitcast(U32).indirect(offsets[:, j0 // 16 : (j0 + n) // 16]))
 
-        gather(0)
+        early_words = keep.tile([P, EARLY], U32, name="early_words", align_bytes=64)
+        gather(early_words, 0, EARLY)
         w1_codes, w1_planes = [], []
         for t in range(PACK):
             codes = keep.tile([P, P], U32, name="w1_codes%d" % t, align_bytes=64)
@@ -96,35 +94,44 @@ def tile_picked_dconv_none_p_kernel(tc, x_words, x_scales, w1, w2_words, w2_scal
             w1_codes.append(codes)
             w1_planes.append(plane)
 
-        def convolve(j0, n):
-            words, plane = picked[j0 // GATHER]
-            cols = slice(j0 % GATHER, j0 % GATHER + n)
+        late_words = keep.tile([P, S - EARLY], U32, name="late_words", tag="shared", align_bytes=64)
+        gather(late_words, EARLY, S - EARLY)
+
+        def convolve(j0, n, carry):
+            words = early_words[:, j0 : j0 + n] if j0 < EARLY else late_words[:, j0 - EARLY : j0 - EARLY + n]
             near = ring.tile([P, PACK, n], F32, name="near")
+            far = ring.tile([P, PACK, n + 4], F32, name="far")
+            if carry is None:
+                nc.vector.memset(far[:, :, 0:2], 0.0)
+            else:
+                nc.vector.tensor_copy(out=far[:, :, 0:2], in_=carry)
             for t in range(PACK):
                 h = hpsum.tile([P, BANK], F32, name="h")
                 nc.tensor.matmul_mx(
                     out=h[:, 0:n],
                     lhsT=w1_codes[t][:].bitcast(FP8X4),
                     lhsT_scale=w1_planes[t][:],
-                    rhs=words[:, cols].bitcast(FP8X4),
-                    rhs_scale=plane[:, cols],
+                    rhs=words.bitcast(FP8X4),
+                    rhs_scale=picked_plane[:, j0 : j0 + n],
                     start=True,
                     stop=True,
                 )
                 for u in range(2):
                     nc.scalar.activation(out=odd[:, u, t, j0 + 1 : j0 + 1 + n], in_=h[:, 0:n], func=COPY, scale=tap[:, t, 2 * u + 1 : 2 * u + 2])
                 nc.vector.scalar_tensor_tensor(out=near[:, t, :], in0=h[:, 0:n], scalar=tap[:, t, 0:1], in1=odd[:, 0, t, j0 : j0 + n], op0=MULT, op1=ADD)
-                nc.vector.scalar_tensor_tensor(out=far[:, t, j0 + 2 : j0 + 2 + n], in0=h[:, 0:n], scalar=tap[:, t, 2:3], in1=odd[:, 1, t, j0 : j0 + n], op0=MULT, op1=ADD)
-            return near
+                nc.vector.scalar_tensor_tensor(out=far[:, t, 2 : 2 + n], in0=h[:, 0:n], scalar=tap[:, t, 2:3], in1=odd[:, 1, t, j0 : j0 + n], op0=MULT, op1=ADD)
+            return near, far
 
-        def join(j0, n, near, engine):
+        def join(n, near, far, share):
             z = zpool.tile([P, n, PACK], BF16, name="z", align_bytes=64)
-            engine.tensor_tensor(
-                out=z[:].rearrange("p (c i) t -> p c t i", i=4),
-                in0=near[:].rearrange("p t (c i) -> p c t i", i=4),
-                in1=far[:, :, j0 : j0 + n].rearrange("p t (c i) -> p c t i", i=4),
-                op=ADD,
-            )
+            for engine, a, b in ((nc.vector, max(share - OVERLAP, 0), n), (nc.gpsimd, 0, share)):
+                if b > a:
+                    engine.tensor_tensor(
+                        out=z[:, a:b, :].rearrange("p (c i) t -> p c t i", i=4),
+                        in0=near[:, :, a:b].rearrange("p t (c i) -> p c t i", i=4),
+                        in1=far[:, :, a:b].rearrange("p t (c i) -> p c t i", i=4),
+                        op=ADD,
+                    )
             return z
 
         def project(j0, n, z):
@@ -148,11 +155,11 @@ def tile_picked_dconv_none_p_kernel(tc, x_words, x_scales, w1, w2_words, w2_scal
 
         starts = [sum(CHUNKS[:c]) for c in range(len(CHUNKS))]
         waiting = None
+        carry = None
         for c, (j0, n) in enumerate(zip(starts, CHUNKS)):
-            if len(picked) < S // GATHER:
-                gather(len(picked))
-            near = convolve(j0, n)
+            near, far = convolve(j0, n, carry)
+            carry = far[:, :, n : n + 2]
             if waiting is not None:
                 project(*waiting)
-            waiting = (j0, n, join(j0, n, near, nc.gpsimd if c < GPSIMD_CHUNKS else nc.vector))
+            waiting = (j0, n, join(n, near, far, GPSIMD_SHARE[c]))
         project(*waiting)

from contextlib import ExitStack

import concourse.mybir as mybir

K, T, S, TAPS, H, N = 512, 2048, 1024, 4, 512, 256
FLOPS = 2 * K * H * S + 2 * H * N * S

F32 = mybir.dt.float32
BF16 = mybir.dt.bfloat16
I32 = mybir.dt.int32
U32 = mybir.dt.uint32
U16 = mybir.dt.uint16
U8 = mybir.dt.uint8
FP8X4 = mybir.dt.float8_e4m3fn_x4
COPY = mybir.ActivationFunctionType.Copy
MULT = mybir.AluOpType.mult
ADD = mybir.AluOpType.add

P = 128
PACK = 4
BANK = 512
EARLY = 640
CHUNKS = [128,256,256,256,128]
GPSIMD_SHARE = [128,176,176,80,0]
OVERLAP = 4
W1_PIECES = [256,128,128]
ROW = S + 8


def load_scale_rows(nc, plane, rows):
    for q in range(4):
        nc.sync.dma_start(out=plane[32 * q : 32 * q + 4, :].bitcast(I32), in_=rows[4 * q : 4 * q + 4, :].bitcast(I32))


def tile_picked_dconv_none_p_kernel(tc, x_words, x_scales, w1, w2_words, w2_scales, taps, offs, out):
    nc = tc.nc
    with ExitStack() as ctx:
        keep = ctx.enter_context(tc.tile_pool(name="keep", bufs=1))
        zpool = ctx.enter_context(tc.tile_pool(name="zpool", bufs=2))
        ring = ctx.enter_context(tc.tile_pool(name="ring", bufs=2))
        hpsum = ctx.enter_context(tc.psum_pool(name="hpsum", bufs=6))
        opsum = ctx.enter_context(tc.psum_pool(name="opsum", bufs=2))

        offsets = keep.tile([P, S // 16], U16, name="offsets")
        x_table = keep.tile([P, T], I32, name="x_table", align_bytes=64)
        x_plane = keep.tile([P, T], U8, name="x_plane", align_bytes=64)
        w2_codes = keep.tile([P, N], I32, name="w2_codes", align_bytes=64)
        w2_plane = keep.tile([P, N], U8, name="w2_plane", align_bytes=64)
        tap = keep.tile([P, PACK, TAPS], F32, name="tap")
        zeros = keep.tile([P, 2, PACK, 1], F32, name="zeros")
        odd = keep.tile([P, 2, PACK, ROW], F32, name="odd")

        nc.vector.memset(x_plane[:].bitcast(I32), 0)
        nc.vector.memset(zeros[:], 0.0)
        nc.vector.memset(w2_plane[:].bitcast(I32), 0)
        nc.scalar.activation(out=odd[:, :, :, 0:1], in_=zeros[:], func=COPY)

        w1_rows = w1.rearrange("(p j) c -> p j c", j=PACK)
        w1_grouped = keep.tile([P, PACK, P, PACK], BF16, name="w1_grouped", tag="shared", align_bytes=64)

        def load_w1_piece(i):
            c0, width = sum(W1_PIECES[:i]), W1_PIECES[i]
            raw = keep.tile([P, PACK, width], F32, name="w1_raw%d" % i)
            nc.sync.dma_start(out=raw[:], in_=w1_rows[:, :, c0 : c0 + width])
            nc.scalar.activation(
                out=w1_grouped[:, :, c0 // PACK : (c0 + width) // PACK, :].rearrange("p t m j -> p m t j"),
                in_=raw[:].rearrange("p j (m t) -> p m t j", t=PACK),
                func=COPY,
            )

        nc.sync.dma_start(offsets[:], offs)
        nc.sync.dma_start(out=tap[:], in_=taps.rearrange("(p t) d -> p t d", t=PACK))
        load_w1_piece(0)
        load_scale_rows(nc, x_plane, x_scales[0])
        nc.sync.dma_start(out=x_table[:], in_=x_words[0].rearrange("p n r -> p (n r)").bitcast(I32))
        for i in range(1, len(W1_PIECES)):
            load_w1_piece(i)
        nc.sync.dma_start(out=w2_codes[:], in_=w2_words[0].rearrange("p n r -> p (n r)").bitcast(I32))
        load_scale_rows(nc, w2_plane, w2_scales[0])

        picked_plane = keep.tile([P, S], U8, name="picked_plane", align_bytes=64)
        nc.vector.tensor_copy(out=picked_plane[:], in_=x_plane[:].indirect(offsets[:]))

        def gather(words, j0, n):
            nc.vector.tensor_copy(out=words[:], in_=x_table[:].bitcast(U32).indirect(offsets[:, j0 // 16 : (j0 + n) // 16]))

        early_words = keep.tile([P, EARLY], U32, name="early_words", align_bytes=64)
        gather(early_words, 0, EARLY)
        w1_codes, w1_planes = [], []
        for t in range(PACK):
            codes = keep.tile([P, P], U32, name="w1_codes%d" % t, align_bytes=64)
            plane = keep.tile([P, P], U8, name="w1_plane%d" % t, align_bytes=64)
            nc.vector.quantize_mx(out=codes[:].bitcast(FP8X4), scales=plane[:], in_=w1_grouped[:, t, :, :].rearrange("p m j -> p (m j)"))
            w1_codes.append(codes)
            w1_planes.append(plane)

        late_words = keep.tile([P, S - EARLY], U32, name="late_words", tag="shared", align_bytes=64)
        gather(late_words, EARLY, S - EARLY)

        def convolve(j0, n, carry):
            words = early_words[:, j0 : j0 + n] if j0 < EARLY else late_words[:, j0 - EARLY : j0 - EARLY + n]
            near = ring.tile([P, PACK, n], F32, name="near")
            far = ring.tile([P, PACK, n + 4], F32, name="far")
            if carry is None:
                nc.vector.memset(far[:, :, 0:2], 0.0)
            else:
                nc.vector.tensor_copy(out=far[:, :, 0:2], in_=carry)
            for t in range(PACK):
                h = hpsum.tile([P, BANK], F32, name="h")
                nc.tensor.matmul_mx(
                    out=h[:, 0:n],
                    lhsT=w1_codes[t][:].bitcast(FP8X4),
                    lhsT_scale=w1_planes[t][:],
                    rhs=words.bitcast(FP8X4),
                    rhs_scale=picked_plane[:, j0 : j0 + n],
                    start=True,
                    stop=True,
                )
                for u in range(2):
                    nc.scalar.activation(out=odd[:, u, t, j0 + 1 : j0 + 1 + n], in_=h[:, 0:n], func=COPY, scale=tap[:, t, 2 * u + 1 : 2 * u + 2])
                nc.vector.scalar_tensor_tensor(out=near[:, t, :], in0=h[:, 0:n], scalar=tap[:, t, 0:1], in1=odd[:, 0, t, j0 : j0 + n], op0=MULT, op1=ADD)
                nc.vector.scalar_tensor_tensor(out=far[:, t, 2 : 2 + n], in0=h[:, 0:n], scalar=tap[:, t, 2:3], in1=odd[:, 1, t, j0 : j0 + n], op0=MULT, op1=ADD)
            return near, far

        def join(n, near, far, share):
            z = zpool.tile([P, n, PACK], BF16, name="z", align_bytes=64)
            for engine, a, b in ((nc.vector, max(share - OVERLAP, 0), n), (nc.gpsimd, 0, share)):
                if b > a:
                    engine.tensor_tensor(
                        out=z[:, a:b, :].rearrange("p (c i) t -> p c t i", i=4),
                        in0=near[:, :, a:b].rearrange("p t (c i) -> p c t i", i=4),
                        in1=far[:, :, a:b].rearrange("p t (c i) -> p c t i", i=4),
                        op=ADD,
                    )
            return z

        def project(j0, n, z):
            codes = ring.tile([P, n], U32, name="z_codes", align_bytes=64)
            plane = ring.tile([P, n], U8, name="z_plane", align_bytes=64)
            nc.vector.quantize_mx(out=codes[:].bitcast(FP8X4), scales=plane[:], in_=z[:].rearrange("p j t -> p (j t)"))
            acc = opsum.tile([P, N // P, BANK // 2], F32, name="acc")
            for m in range(N // P):
                nc.tensor.matmul_mx(
                    out=acc[:, m, 0:n],
                    lhsT=w2_codes[:, m * P : (m + 1) * P].bitcast(FP8X4),
                    lhsT_scale=w2_plane[:, m * P : (m + 1) * P],
                    rhs=codes[:].bitcast(FP8X4),
                    rhs_scale=plane[:],
                    start=True,
                    stop=True,
                )
            result = ring.tile([P, N // P, n], F32, name="result")
            nc.scalar.activation(out=result[:], in_=acc[:, :, 0:n], func=COPY)
            nc.sync.dma_start(out=out.rearrange("(m p) j -> p m j", p=P)[:, :, j0 : j0 + n], in_=result[:])

        starts = [sum(CHUNKS[:c]) for c in range(len(CHUNKS))]
        waiting = None
        carry = None
        for c, (j0, n) in enumerate(zip(starts, CHUNKS)):
            near, far = convolve(j0, n, carry)
            carry = far[:, :, n : n + 2]
            if waiting is not None:
                project(*waiting)
            waiting = (j0, n, join(n, near, far, GPSIMD_SHARE[c]))
        project(*waiting)
